import numpy as np
import ml_dtypes


def mxq(x, axis, fmt="e4m3"):
    dtype, down = {"e4m3": (ml_dtypes.float8_e4m3fn, 7), "e5m2": (ml_dtypes.float8_e5m2, 14)}[fmt]
    v = np.moveaxis(np.asarray(x, np.float32).astype(ml_dtypes.bfloat16).astype(np.float64), axis, -1)
    blocks = v.reshape(v.shape[:-1] + (-1, 32))
    amax = np.abs(blocks).max(-1, keepdims=True)
    byte = np.maximum(np.where(amax > 0, np.frexp(amax)[1] - 1 + 127, 0) - down, 1)
    scale = np.exp2(byte - 127.0)
    codes = (blocks / scale).astype(np.float32).astype(dtype).astype(np.float64)
    return np.moveaxis((codes * scale).reshape(v.shape), -1, axis)


WIDE = False


def mx_kscale(k):
    if not WIDE:
        return np.ones(k)
    levels = np.array([30, -30])
    if k % 512:
        return np.exp2(np.random.permutation(np.resize(levels, k // 32))).repeat(32)
    a = np.empty((k // 512, 16))
    for p in range(k // 512):
        a[p, :8] = np.random.permutation(np.resize(levels, 8))
        for g in range(8):
            far = levels[np.abs(levels - a[p, g]) >= 10]
            a[p, g + 8] = far[np.random.randint(len(far))]
    return np.exp2(a.ravel()).repeat(32)


BF16 = ml_dtypes.bfloat16


def bf(x):
    return np.asarray(x, np.float32).astype(BF16)


def f64(x):
    return np.asarray(x).astype(np.float64)


M, P, T, N = 1024, 512, 1536, 2048

DF = 5.0


def setup_inputs():
    s, t = mx_kscale(P), mx_kscale(T)
    h_pre = np.random.standard_normal((M, P)) * s
    h_late = np.random.standard_t(DF, (M, T)) * np.sqrt((DF - 2.0) / DF) * t
    w_pre = np.random.standard_normal((P, N)) / np.sqrt(P) / s[:, None]
    w_late = np.random.standard_normal((T, N)) / np.sqrt(T) / t[:, None]
    return {"h": bf(np.concatenate([h_pre, h_late], axis=1)),
            "w": bf(np.concatenate([w_pre, w_late], axis=0)),
            "b": bf(0.3 * np.random.standard_normal(N)),
            "beta": bf(1.0 + 0.1 * np.random.standard_normal(M))}


def reference(h, w, b, beta):
    h, w = f64(h), f64(w)
    short = mxq(h[:, :P], 1, "e4m3") @ mxq(w[:P], 0, "e4m3")
    late = mxq(h[:, P:], 1, "e5m2") @ mxq(w[P:], 0, "e4m3")
    diff = late + f64(b)
    full = short + diff
    gap = np.tanh(f64(beta)[:, None] * diff)
    return full, gap

@@ -1,0 +1,227 @@
+from contextlib import ExitStack
+
+import concourse.mybir as mybir
+from concourse.masks import make_identity
+
+M, K, N = 1024, 2048, 2048
+FLOPS = 2 * M * K * N
+
+F32 = mybir.dt.float32
+BF16 = mybir.dt.bfloat16
+U32 = mybir.dt.uint32
+U8 = mybir.dt.uint8
+E4M3 = mybir.dt.float8_e4m3fn_x4
+E5M2 = mybir.dt.float8_e5m2_x4
+ACT = mybir.ActivationFunctionType
+ADD = mybir.AluOpType.add
+
+P = 128
+PACK = 4
+K_PASS = P * PACK
+COLS = 512
+TILES = M // P
+CHUNKS = N // COLS
+UNITS = TILES * CHUNKS
+PASS_ORDER = (1, 2, 3, 0)
+VECTOR_COLS = (320, 256, 64, 64)
+AHEAD = 3
+
+
+def tile_matryoshka_softened_gap_s2_kernel(tc, h, w, b, beta, out_0, out_1):
+    nc = tc.nc
+    h_rows = h.rearrange("(p i) k -> p i k", i=TILES)
+    full_rows = out_0.rearrange("(p i) n -> p i n", i=TILES)
+    gap_rows = out_1.rearrange("(p i) n -> p i n", i=TILES)
+
+    with ExitStack() as ctx:
+        keep = ctx.enter_context(tc.tile_pool(name="keep", bufs=1))
+        stage = ctx.enter_context(tc.tile_pool(name="stage", bufs=1))
+        psum = ctx.enter_context(tc.psum_pool(name="psum", bufs=1))
+        ctx.enter_context(tc.manual_schedule())
+
+        h_raw, w_raw, h_turned, h_grouped, w_grouped = {}, {}, {}, {}, {}
+        h_codes, h_scales, w_codes, w_scales = {}, {}, {}, {}
+        late, short, diff, full, gap = {}, {}, {}, {}, {}
+
+        def load_h(i):
+            h_raw[i] = stage.tile([P, K], BF16, name="h_raw", bufs=5)
+            nc.sync.dma_start(out=h_raw[i][:], in_=h_rows[:, i, :])
+
+        def load_w(g, c0, count):
+            raw = keep.tile([P, PACK, count * COLS], BF16, name="w_raw_%d_%d" % (g, c0))
+            rows = w[g * K_PASS : (g + 1) * K_PASS, c0 * COLS : (c0 + count) * COLS]
+            nc.sync.dma_start(out=raw[:], in_=rows.rearrange("(p t) n -> p t n", t=PACK))
+            for c in range(count):
+                w_raw[g, c0 + c] = raw[:, :, c * COLS : (c + 1) * COLS]
+
+        b_raw = keep.tile([P, N // P], BF16)
+        nc.sync.dma_start(out=b_raw[:], in_=b.rearrange("(p j) -> p j", p=P))
+        beta_raw = keep.tile([P, TILES], BF16)
+        nc.sync.dma_start(out=beta_raw[:], in_=beta.rearrange("(p i) -> p i", i=TILES))
+        for n, g in enumerate(PASS_ORDER):
+            load_w(g, 0, 1)
+            if n < AHEAD:
+                load_h(n)
+        load_w(1, 1, 1)
+        load_h(3)
+        load_w(2, 1, 1)
+        load_h(4)
+        load_h(5)
+        load_w(3, 1, 1)
+        load_h(6)
+        load_w(0, 1, 1)
+        load_h(7)
+        for g in PASS_ORDER:
+            load_w(g, 2, 2)
+
+        ident = keep.tile([P, P], F32)
+        make_identity(nc, ident[:])
+
+        zero = keep.tile([P, 1], F32)
+        nc.vector.memset(zero[:], 0.0)
+        zero_bias = keep.tile([P, 1], F32)
+        nc.scalar.activation(out=zero_bias[:], in_=zero[:], func=ACT.Tanh)
+
+        beta_f32 = keep.tile([P, TILES], F32)
+        nc.vector.tensor_copy(out=beta_f32[:], in_=beta_raw[:])
+
+        b_all = keep.tile([P, N], BF16)
+        b_words = b_raw[:].bitcast(F32)
+        b_all_words = b_all[:].bitcast(F32).rearrange("m (p u) -> m p u", p=P)
+        for half in range(2):
+            bank = psum.tile([P, 4, P], F32, name="turned", bufs=2)
+            for u in range(4):
+                word = 4 * half + u
+                nc.tensor.transpose(bank[:, u, :], b_words[:, word : word + 1].to_broadcast([P, P]), ident[:])
+            src = bank[:].rearrange("m u p -> m p u")
+            dst = b_all_words[:, :, 4 * half : 4 * half + 4]
+            nc.vector.tensor_copy(out=dst, in_=src)
+
+        def turn_h(i):
+            words = h_raw[i][:].bitcast(F32)
+            for half in range(2):
+                bank = psum.tile([P, 2, 2, P], F32, name="turned", bufs=2)
+                h_turned[i, half] = bank
+                for slot in range(2):
+                    g = PASS_ORDER[2 * half + slot]
+                    for u in range(2):
+                        nc.tensor.transpose(bank[:, slot, u, :], words[:, 256 * g + u : 256 * (g + 1) : 2], ident[:])
+
+        def group_h(i):
+            h_grouped[i] = stage.tile([P, K], BF16, name="h_grouped", bufs=2, align_bytes=64)
+            words = h_grouped[i][:].bitcast(F32).rearrange("p (s r u) -> p s r u", s=4, u=2)
+            for half in range(2):
+                nc.scalar.copy(
+                    out=words[:, 2 * half : 2 * half + 2, :, :],
+                    in_=h_turned[i, half][:].rearrange("p s u r -> p s r u"),
+                )
+
+        def quantize_h(i):
+            h_codes[i] = keep.tile([P, 4 * P], U32, name="h_codes_%d" % i, align_bytes=64)
+            h_scales[i] = keep.tile([P, 4 * P], U8, name="h_scales_%d" % i, align_bytes=64)
+            for s0, s1, fmt in ((0, 2, E5M2), (2, 3, E5M2), (3, 4, E4M3)):
+                nc.vector.quantize_mx(
+                    out=h_codes[i][:, s0 * P : s1 * P].bitcast(fmt),
+                    scales=h_scales[i][:, s0 * P : s1 * P],
+                    in_=h_grouped[i][:, s0 * K_PASS : s1 * K_PASS],
+                )
+
+        def group_w(g, c, n0, n1, copy):
+            if (g, c) not in w_grouped:
+                w_grouped[g, c] = stage.tile([P, COLS, PACK], BF16, name="w_grouped", bufs=3, align_bytes=64)
+            copy(
+                out=w_grouped[g, c][:, n0:n1, :].rearrange("p (c i) t -> p c t i", i=4),
+                in_=w_raw[g, c][:, :, n0:n1].rearrange("p t (c i) -> p c t i", i=4),
+            )
+
+        def quantize_w(g, c):
+            w_codes[g, c] = keep.tile([P, COLS], U32, name="w_codes_%d_%d" % (g, c), align_bytes=64)
+            w_scales[g, c] = keep.tile([P, COLS], U8, name="w_scales_%d_%d" % (g, c), align_bytes=64)
+            nc.vector.quantize_mx(
+                out=w_codes[g, c][:].bitcast(E4M3),
+                scales=w_scales[g, c][:],
+                in_=w_grouped[g, c][:].rearrange("p n t -> p (n t)"),
+            )
+
+        def multiply(s):
+            c, i = divmod(s, TILES)
+            late[s] = psum.tile([P, COLS], F32, name="late", bufs=3)
+            short[s] = psum.tile([P, COLS], F32, name="short", bufs=3)
+            for slot, g in enumerate(PASS_ORDER):
+                cols = slice(slot * P, (slot + 1) * P)
+                nc.tensor.matmul_mx(
+                    out=short[s][:] if g == 0 else late[s][:],
+                    lhsT=h_codes[i][:, cols].bitcast(E4M3 if g == 0 else E5M2),
+                    lhsT_scale=h_scales[i][:, cols],
+                    rhs=w_codes[g, c][:].bitcast(E4M3),
+                    rhs_scale=w_scales[g, c][:],
+                    start=g in (0, 1),
+                    stop=g in (0, 3),
+                )
+
+        def add_bias(s):
+            c = s // TILES
+            diff[s] = stage.tile([P, COLS], F32, name="diff", bufs=4)
+            nc.vector.tensor_tensor(out=diff[s][:], in0=late[s][:], in1=b_all[:, c * COLS : (c + 1) * COLS], op=ADD)
+
+        def store_group(s):
+            if s >= UNITS - 2:
+                return s, 1
+            return s - s % 2, 2
+
+        def finish(s):
+            c, i = divmod(s, TILES)
+            first, count = store_group(s)
+            if s == first:
+                full[first] = stage.tile([P, count, COLS], F32, name="result", bufs=14)
+                gap[first] = stage.tile([P, count, COLS], F32, name="result", bufs=14)
+            nc.vector.tensor_tensor(out=full[first][:, s - first, :], in0=short[s][:], in1=diff[s][:], op=ADD)
+            nc.scalar.activation(
+                out=gap[first][:, s - first, :],
+                in_=diff[s][:],
+                func=ACT.Tanh,
+                scale=beta_f32[:, i : i + 1],
+                bias=zero_bias[:],
+            )
+            if s == first + count - 1:
+                tiles = slice(i - count + 1, i + 1)
+                cols = slice(c * COLS, (c + 1) * COLS)
+                nc.sync.dma_start(out=full_rows[:, tiles, cols], in_=full[first][:])
+                nc.sync.dma_start(out=gap_rows[:, tiles, cols], in_=gap[first][:])
+
+        for n, g in enumerate(PASS_ORDER):
+            group_w(g, 0, 0, VECTOR_COLS[0], nc.vector.tensor_copy)
+            group_w(g, 0, VECTOR_COLS[0], COLS, nc.scalar.copy)
+            if n > 0:
+                quantize_w(PASS_ORDER[n - 1], 0)
+                quantize_h(n - 1)
+            if n < AHEAD:
+                turn_h(n)
+                group_h(n)
+        quantize_w(PASS_ORDER[-1], 0)
+        multiply(0)
+
+        pieces = [(g, c) for c in range(1, CHUNKS) for g in PASS_ORDER]
+        for s in range(-2, UNITS + 1):
+            j, phase = divmod(s + 2, 2)
+            if phase == 1 and 0 <= j - 1 < len(pieces):
+                quantize_w(*pieces[j - 1])
+            if 0 <= s < TILES - AHEAD:
+                turn_h(s + AHEAD)
+            if 0 < s + 1 < UNITS:
+                multiply(s + 1)
+            if j < len(pieces):
+                g, c = pieces[j]
+                split = VECTOR_COLS[c]
+                width = (COLS - split) // 2
+                group_w(g, c, split + phase * width, split + (phase + 1) * width, nc.scalar.copy)
+            if 0 <= s < UNITS:
+                add_bias(s)
+            if 1 <= s <= TILES - AHEAD:
+                quantize_h(s + AHEAD - 1)
+            if j < len(pieces) and phase == 0:
+                group_w(g, c, 0, split, nc.vector.tensor_copy)
+            if s > 0:
+                finish(s - 1)
+            if 0 <= s < TILES - AHEAD:
+                group_h(s + AHEAD)

@@ -23,7 +23,8 @@ TILES = M // P
 CHUNKS = N // COLS
 UNITS = TILES * CHUNKS
 PASS_ORDER = (1, 2, 3, 0)
-VECTOR_COLS = (320, 256, 64, 64)
+VECTOR_COLS = (320, 128, 0, 0)
+GPSIMD_COLS = (0, 128, 160, 160)
 AHEAD = 3
 
 
@@ -128,10 +129,20 @@ def tile_matryoshka_softened_gap_s2_kernel(tc, h, w, b, beta, out_0, out_1):
 
         def group_w(g, c, n0, n1, copy):
             if (g, c) not in w_grouped:
-                w_grouped[g, c] = stage.tile([P, COLS, PACK], BF16, name="w_grouped", bufs=3, align_bytes=64)
+                w_grouped[g, c] = stage.tile([P, COLS, PACK], BF16, name="w_grouped", bufs=2, align_bytes=64)
             copy(
                 out=w_grouped[g, c][:, n0:n1, :].rearrange("p (c i) t -> p c t i", i=4),
                 in_=w_raw[g, c][:, :, n0:n1].rearrange("p t (c i) -> p c t i", i=4),
+            )
+
+        def group_w_gpsimd(g, c, n0, n1):
+            nc.gpsimd.tensor_scalar(
+                out=w_grouped[g, c][:, n0:n1, :],
+                in0=w_raw[g, c][:, :, n0:n1].rearrange("p t n -> p n t"),
+                scalar1=1.0,
+                scalar2=0.0,
+                op0=mybir.AluOpType.mult,
+                op1=ADD,
             )
 
         def quantize_w(g, c):
@@ -213,13 +224,15 @@ def tile_matryoshka_softened_gap_s2_kernel(tc, h, w, b, beta, out_0, out_1):
             if j < len(pieces):
                 g, c = pieces[j]
                 split = VECTOR_COLS[c]
-                width = (COLS - split) // 2
+                width = (COLS - split - GPSIMD_COLS[c]) // 2
                 group_w(g, c, split + phase * width, split + (phase + 1) * width, nc.scalar.copy)
+                if phase == 0:
+                    group_w_gpsimd(g, c, COLS - GPSIMD_COLS[c], COLS)
             if 0 <= s < UNITS:
                 add_bias(s)
             if 1 <= s <= TILES - AHEAD:
                 quantize_h(s + AHEAD - 1)
-            if j < len(pieces) and phase == 0:
+            if j < len(pieces) and phase == 0 and split > 0:
                 group_w(g, c, 0, split, nc.vector.tensor_copy)
             if s > 0:
                 finish(s - 1)

from contextlib import ExitStack

import concourse.mybir as mybir
from concourse.masks import make_identity

M, K, N = 1024, 2048, 2048
FLOPS = 2 * M * K * N

F32 = mybir.dt.float32
BF16 = mybir.dt.bfloat16
U32 = mybir.dt.uint32
U8 = mybir.dt.uint8
E4M3 = mybir.dt.float8_e4m3fn_x4
E5M2 = mybir.dt.float8_e5m2_x4
ACT = mybir.ActivationFunctionType
ADD = mybir.AluOpType.add

P = 128
PACK = 4
K_PASS = P * PACK
COLS = 512
TILES = M // P
CHUNKS = N // COLS
UNITS = TILES * CHUNKS
PASS_ORDER = (1, 2, 3, 0)
VECTOR_COLS = (320, 128, 0, 0)
GPSIMD_COLS = (0, 128, 160, 160)
AHEAD = 3


def tile_matryoshka_softened_gap_s2_kernel(tc, h, w, b, beta, out_0, out_1):
    nc = tc.nc
    h_rows = h.rearrange("(p i) k -> p i k", i=TILES)
    full_rows = out_0.rearrange("(p i) n -> p i n", i=TILES)
    gap_rows = out_1.rearrange("(p i) n -> p i n", i=TILES)

    with ExitStack() as ctx:
        keep = ctx.enter_context(tc.tile_pool(name="keep", bufs=1))
        stage = ctx.enter_context(tc.tile_pool(name="stage", bufs=1))
        psum = ctx.enter_context(tc.psum_pool(name="psum", bufs=1))
        ctx.enter_context(tc.manual_schedule())

        h_raw, w_raw, h_turned, h_grouped, w_grouped = {}, {}, {}, {}, {}
        h_codes, h_scales, w_codes, w_scales = {}, {}, {}, {}
        late, short, diff, full, gap = {}, {}, {}, {}, {}

        def load_h(i):
            h_raw[i] = stage.tile([P, K], BF16, name="h_raw", bufs=5)
            nc.sync.dma_start(out=h_raw[i][:], in_=h_rows[:, i, :])

        def load_w(g, c0, count):
            raw = keep.tile([P, PACK, count * COLS], BF16, name="w_raw_%d_%d" % (g, c0))
            rows = w[g * K_PASS : (g + 1) * K_PASS, c0 * COLS : (c0 + count) * COLS]
            nc.sync.dma_start(out=raw[:], in_=rows.rearrange("(p t) n -> p t n", t=PACK))
            for c in range(count):
                w_raw[g, c0 + c] = raw[:, :, c * COLS : (c + 1) * COLS]

        b_raw = keep.tile([P, N // P], BF16)
        nc.sync.dma_start(out=b_raw[:], in_=b.rearrange("(p j) -> p j", p=P))
        beta_raw = keep.tile([P, TILES], BF16)
        nc.sync.dma_start(out=beta_raw[:], in_=beta.rearrange("(p i) -> p i", i=TILES))
        for n, g in enumerate(PASS_ORDER):
            load_w(g, 0, 1)
            if n < AHEAD:
                load_h(n)
        load_w(1, 1, 1)
        load_h(3)
        load_w(2, 1, 1)
        load_h(4)
        load_h(5)
        load_w(3, 1, 1)
        load_h(6)
        load_w(0, 1, 1)
        load_h(7)
        for g in PASS_ORDER:
            load_w(g, 2, 2)

        ident = keep.tile([P, P], F32)
        make_identity(nc, ident[:])

        zero = keep.tile([P, 1], F32)
        nc.vector.memset(zero[:], 0.0)
        zero_bias = keep.tile([P, 1], F32)
        nc.scalar.activation(out=zero_bias[:], in_=zero[:], func=ACT.Tanh)

        beta_f32 = keep.tile([P, TILES], F32)
        nc.vector.tensor_copy(out=beta_f32[:], in_=beta_raw[:])

        b_all = keep.tile([P, N], BF16)
        b_words = b_raw[:].bitcast(F32)
        b_all_words = b_all[:].bitcast(F32).rearrange("m (p u) -> m p u", p=P)
        for half in range(2):
            bank = psum.tile([P, 4, P], F32, name="turned", bufs=2)
            for u in range(4):
                word = 4 * half + u
                nc.tensor.transpose(bank[:, u, :], b_words[:, word : word + 1].to_broadcast([P, P]), ident[:])
            src = bank[:].rearrange("m u p -> m p u")
            dst = b_all_words[:, :, 4 * half : 4 * half + 4]
            nc.vector.tensor_copy(out=dst, in_=src)

        def turn_h(i):
            words = h_raw[i][:].bitcast(F32)
            for half in range(2):
                bank = psum.tile([P, 2, 2, P], F32, name="turned", bufs=2)
                h_turned[i, half] = bank
                for slot in range(2):
                    g = PASS_ORDER[2 * half + slot]
                    for u in range(2):
                        nc.tensor.transpose(bank[:, slot, u, :], words[:, 256 * g + u : 256 * (g + 1) : 2], ident[:])

        def group_h(i):
            h_grouped[i] = stage.tile([P, K], BF16, name="h_grouped", bufs=2, align_bytes=64)
            words = h_grouped[i][:].bitcast(F32).rearrange("p (s r u) -> p s r u", s=4, u=2)
            for half in range(2):
                nc.scalar.copy(
                    out=words[:, 2 * half : 2 * half + 2, :, :],
                    in_=h_turned[i, half][:].rearrange("p s u r -> p s r u"),
                )

        def quantize_h(i):
            h_codes[i] = keep.tile([P, 4 * P], U32, name="h_codes_%d" % i, align_bytes=64)
            h_scales[i] = keep.tile([P, 4 * P], U8, name="h_scales_%d" % i, align_bytes=64)
            for s0, s1, fmt in ((0, 2, E5M2), (2, 3, E5M2), (3, 4, E4M3)):
                nc.vector.quantize_mx(
                    out=h_codes[i][:, s0 * P : s1 * P].bitcast(fmt),
                    scales=h_scales[i][:, s0 * P : s1 * P],
                    in_=h_grouped[i][:, s0 * K_PASS : s1 * K_PASS],
                )

        def group_w(g, c, n0, n1, copy):
            if (g, c) not in w_grouped:
                w_grouped[g, c] = stage.tile([P, COLS, PACK], BF16, name="w_grouped", bufs=2, align_bytes=64)
            copy(
                out=w_grouped[g, c][:, n0:n1, :].rearrange("p (c i) t -> p c t i", i=4),
                in_=w_raw[g, c][:, :, n0:n1].rearrange("p t (c i) -> p c t i", i=4),
            )

        def group_w_gpsimd(g, c, n0, n1):
            nc.gpsimd.tensor_scalar(
                out=w_grouped[g, c][:, n0:n1, :],
                in0=w_raw[g, c][:, :, n0:n1].rearrange("p t n -> p n t"),
                scalar1=1.0,
                scalar2=0.0,
                op0=mybir.AluOpType.mult,
                op1=ADD,
            )

        def quantize_w(g, c):
            w_codes[g, c] = keep.tile([P, COLS], U32, name="w_codes_%d_%d" % (g, c), align_bytes=64)
            w_scales[g, c] = keep.tile([P, COLS], U8, name="w_scales_%d_%d" % (g, c), align_bytes=64)
            nc.vector.quantize_mx(
                out=w_codes[g, c][:].bitcast(E4M3),
                scales=w_scales[g, c][:],
                in_=w_grouped[g, c][:].rearrange("p n t -> p (n t)"),
            )

        def multiply(s):
            c, i = divmod(s, TILES)
            late[s] = psum.tile([P, COLS], F32, name="late", bufs=3)
            short[s] = psum.tile([P, COLS], F32, name="short", bufs=3)
            for slot, g in enumerate(PASS_ORDER):
                cols = slice(slot * P, (slot + 1) * P)
                nc.tensor.matmul_mx(
                    out=short[s][:] if g == 0 else late[s][:],
                    lhsT=h_codes[i][:, cols].bitcast(E4M3 if g == 0 else E5M2),
                    lhsT_scale=h_scales[i][:, cols],
                    rhs=w_codes[g, c][:].bitcast(E4M3),
                    rhs_scale=w_scales[g, c][:],
                    start=g in (0, 1),
                    stop=g in (0, 3),
                )

        def add_bias(s):
            c = s // TILES
            diff[s] = stage.tile([P, COLS], F32, name="diff", bufs=4)
            nc.vector.tensor_tensor(out=diff[s][:], in0=late[s][:], in1=b_all[:, c * COLS : (c + 1) * COLS], op=ADD)

        def store_group(s):
            if s >= UNITS - 2:
                return s, 1
            return s - s % 2, 2

        def finish(s):
            c, i = divmod(s, TILES)
            first, count = store_group(s)
            if s == first:
                full[first] = stage.tile([P, count, COLS], F32, name="result", bufs=14)
                gap[first] = stage.tile([P, count, COLS], F32, name="result", bufs=14)
            nc.vector.tensor_tensor(out=full[first][:, s - first, :], in0=short[s][:], in1=diff[s][:], op=ADD)
            nc.scalar.activation(
                out=gap[first][:, s - first, :],
                in_=diff[s][:],
                func=ACT.Tanh,
                scale=beta_f32[:, i : i + 1],
                bias=zero_bias[:],
            )
            if s == first + count - 1:
                tiles = slice(i - count + 1, i + 1)
                cols = slice(c * COLS, (c + 1) * COLS)
                nc.sync.dma_start(out=full_rows[:, tiles, cols], in_=full[first][:])
                nc.sync.dma_start(out=gap_rows[:, tiles, cols], in_=gap[first][:])

        for n, g in enumerate(PASS_ORDER):
            group_w(g, 0, 0, VECTOR_COLS[0], nc.vector.tensor_copy)
            group_w(g, 0, VECTOR_COLS[0], COLS, nc.scalar.copy)
            if n > 0:
                quantize_w(PASS_ORDER[n - 1], 0)
                quantize_h(n - 1)
            if n < AHEAD:
                turn_h(n)
                group_h(n)
        quantize_w(PASS_ORDER[-1], 0)
        multiply(0)

        pieces = [(g, c) for c in range(1, CHUNKS) for g in PASS_ORDER]
        for s in range(-2, UNITS + 1):
            j, phase = divmod(s + 2, 2)
            if phase == 1 and 0 <= j - 1 < len(pieces):
                quantize_w(*pieces[j - 1])
            if 0 <= s < TILES - AHEAD:
                turn_h(s + AHEAD)
            if 0 < s + 1 < UNITS:
                multiply(s + 1)
            if j < len(pieces):
                g, c = pieces[j]
                split = VECTOR_COLS[c]
                width = (COLS - split - GPSIMD_COLS[c]) // 2
                group_w(g, c, split + phase * width, split + (phase + 1) * width, nc.scalar.copy)
                if phase == 0:
                    group_w_gpsimd(g, c, COLS - GPSIMD_COLS[c], COLS)
            if 0 <= s < UNITS:
                add_bias(s)
            if 1 <= s <= TILES - AHEAD:
                quantize_h(s + AHEAD - 1)
            if j < len(pieces) and phase == 0 and split > 0:
                group_w(g, c, 0, split, nc.vector.tensor_copy)
            if s > 0:
                finish(s - 1)
            if 0 <= s < TILES - AHEAD:
                group_h(s + AHEAD)
